import numpy as np
import ml_dtypes


def mxq(x, axis, fmt="e4m3"):
    dtype, down = {"e4m3": (ml_dtypes.float8_e4m3fn, 7), "e5m2": (ml_dtypes.float8_e5m2, 14)}[fmt]
    v = np.moveaxis(np.asarray(x, np.float32).astype(ml_dtypes.bfloat16).astype(np.float64), axis, -1)
    blocks = v.reshape(v.shape[:-1] + (-1, 32))
    amax = np.abs(blocks).max(-1, keepdims=True)
    byte = np.maximum(np.where(amax > 0, np.frexp(amax)[1] - 1 + 127, 0) - down, 1)
    scale = np.exp2(byte - 127.0)
    codes = (blocks / scale).astype(np.float32).astype(dtype).astype(np.float64)
    return np.moveaxis((codes * scale).reshape(v.shape), -1, axis)


WIDE = False


def mx_kscale(k):
    if not WIDE:
        return np.ones(k)
    levels = np.array([10, -10, 5, -5, 0])
    if k % 512:
        return np.exp2(np.random.permutation(np.resize(levels, k // 32))).repeat(32)
    a = np.empty((k // 512, 16))
    for p in range(k // 512):
        a[p, :8] = np.random.permutation(np.resize(levels, 8))
        for g in range(8):
            far = levels[np.abs(levels - a[p, g]) >= 10]
            a[p, g + 8] = far[np.random.randint(len(far))]
    return np.exp2(a.ravel()).repeat(32)


def f64(x):
    return np.asarray(x).astype(np.float64)


def striped(idx):
    return np.tile(idx.reshape(-1, 16).T, (8, 1)).astype(np.uint16)


def unstriped(offs):
    return offs[:16].T.reshape(-1).astype(np.int64)


def relu(v):
    return np.maximum(v, 0.0)


K, T, S, H, N = 1024, 2048, 1024, 512, 128


def setup_inputs():
    n = np.random.standard_normal
    s = mx_kscale(K)[:, None]
    u = mx_kscale(H)
    return {
        "xT": (n((K, T)) * s).astype(np.float32),
        "w1": (n((K, H)) / np.sqrt(K) / s * u).astype(np.float32),
        "w2": (n((H, N)) / np.sqrt(H) / u[:, None]).astype(np.float32),
        "offs": striped(np.random.permutation(T)[:S]),
    }


def reference(xT, w1, w2, offs):
    xq = mxq(f64(xT)[:, unstriped(offs)], 0, "e4m3")
    h = relu(mxq(f64(w1), 0, "e4m3").T @ xq)
    z = h - h.mean(axis=1, keepdims=True)
    return mxq(f64(w2), 0, "e4m3").T @ mxq(z, 0, "e4m3")

@@ -1,0 +1,264 @@
+from contextlib import ExitStack
+
+import concourse.mybir as mybir
+
+K, T, S, H, N = 1024, 2048, 1024, 512, 128
+FLOPS = 2 * K * H * S + 2 * H * N * S
+
+F32 = mybir.dt.float32
+BF16 = mybir.dt.bfloat16
+I32 = mybir.dt.int32
+U32 = mybir.dt.uint32
+U16 = mybir.dt.uint16
+U8 = mybir.dt.uint8
+FP8X4 = mybir.dt.float8_e4m3fn_x4
+ALU = mybir.AluOpType
+ACT = mybir.ActivationFunctionType
+
+P = 128
+PACK = 4
+HALF = 512
+QUART = 256
+
+
+def tile_picked_deepset_relu_e_kernel(tc, xT, w1, w2, offs, out):
+    nc = tc.nc
+    x_rows = xT.rearrange("(g p u e) t -> g u p e t", g=2, p=P, u=2, e=2)
+    w1_rows = w1.rearrange("(g p j) c -> g p j c", g=2, p=P, j=PACK)
+    w2_rows = w2.rearrange("(p j) n -> p j n", j=PACK)
+
+    with ExitStack() as ctx:
+        keep = ctx.enter_context(tc.tile_pool(name="keep", bufs=1))
+        psum = ctx.enter_context(tc.psum_pool(name="psum", bufs=1))
+
+        def sbuf(name, shape, dtype):
+            return keep.tile(shape, dtype, name=name, align_bytes=64)
+
+        offsets = keep.tile([P, S // 16], U16, name="offsets")
+
+        x_raw = {}
+
+        def load_x(g, u, t0, t1):
+            raw = sbuf("x_raw_%d_%d_%d" % (g, u, t0), [P, 2, t1 - t0], F32)
+            nc.sync.dma_start(out=raw[:], in_=x_rows[g, u][:, :, t0:t1])
+            x_raw[(g, u, t0)] = raw
+
+        w1_raw = [sbuf("w1_raw_%d" % g, [P, PACK, H], F32) for g in range(2)]
+        w2_raw = sbuf("w2_raw", [P, PACK, N], F32)
+
+        load_x(0, 0, 0, 1024)
+        nc.sync.dma_start(offsets[:], offs)
+        load_x(0, 0, 1024, 2048)
+        load_x(0, 1, 0, 1024)
+        load_x(0, 1, 1024, 2048)
+        load_x(1, 0, 0, 1024)
+        load_x(1, 0, 1024, 2048)
+        load_x(1, 1, 0, 1024)
+        nc.sync.dma_start(out=w1_raw[0][:], in_=w1_rows[0])
+        load_x(1, 1, 1024, 1536)
+        load_x(1, 1, 1536, 2048)
+        nc.sync.dma_start(out=w2_raw[:], in_=w2_rows)
+        nc.sync.dma_start(out=w1_raw[1][:], in_=w1_rows[1])
+
+        pairs = {(g, u): sbuf("pairs_%d_%d" % (g, u), [P, 2 * T], BF16) for g in range(2) for u in range(2)}
+
+        def cast_copy(engine, dst, src):
+            if engine == "v":
+                nc.vector.tensor_copy(out=dst, in_=src)
+            else:
+                nc.scalar.activation(out=dst, in_=src, func=ACT.Copy)
+
+        def cast_x(engine, g, u, t0, a, b):
+            dst = pairs[(g, u)][:, 2 * a : 2 * b].rearrange("p (t e) -> p t e", e=2)
+            src = x_raw[(g, u, t0)][:, :, a - t0 : b - t0].rearrange("p e t -> p t e")
+            cast_copy(engine, dst, src)
+
+        picked = {(g, q): sbuf("picked_%d_%d" % (g, q), [P, 2, QUART], U32) for g in range(2) for q in range(4)}
+        woven = {(g, h): sbuf("woven_%d_%d" % (g, h), [P, PACK * HALF], BF16) for g in range(2) for h in range(2)}
+        x_codes = {(g, h): sbuf("x_codes_%d_%d" % (g, h), [P, HALF], U32) for g, h in ((0, 0), (0, 1), (1, 0))}
+        x_scales = {(g, h): sbuf("x_scales_%d_%d" % (g, h), [P, HALF], U8) for g in range(2) for h in range(2)}
+
+        def gather(g, u, q):
+            window = pairs[(g, u)][:].bitcast(U32)
+            cols = QUART // 16
+            nc.vector.tensor_copy(out=picked[(g, q)][:, u, :], in_=window.indirect(offsets[:, q * cols : (q + 1) * cols]))
+
+        def weave(engine, g, q):
+            h, r = divmod(q, 2)
+            dst = woven[(g, h)][:, r * PACK * QUART : (r + 1) * PACK * QUART]
+            src = picked[(g, q)][:]
+            if engine == "v":
+                nc.vector.tensor_copy(
+                    out=dst.bitcast(I32).rearrange("p (n u) -> p n u", u=2),
+                    in_=src.bitcast(I32).rearrange("p u n -> p n u"),
+                )
+            else:
+                nc.scalar.copy(
+                    out=dst.bitcast(U32).rearrange("p (n u) -> p n u", u=2),
+                    in_=src.rearrange("p u n -> p n u"),
+                )
+
+        def quantize(codes, scales, values):
+            nc.vector.quantize_mx(out=codes.bitcast(FP8X4), scales=scales, in_=values)
+
+        def quantize_x(g, h):
+            quantize(x_codes[(g, h)][:], x_scales[(g, h)][:], woven[(g, h)][:])
+
+        w1_bf = {(g, d): sbuf("w1_bf_%d_%d" % (g, d), [P, 2 * P * PACK], BF16) for g in range(2) for d in range(2)}
+        w1_codes = {(g, d): sbuf("w1_codes_%d_%d" % (g, d), [P, 2 * P], U32) for g in range(2) for d in range(2)}
+        w1_scales = {(g, d): sbuf("w1_scales_%d_%d" % (g, d), [P, 2 * P], U8) for g in range(2) for d in range(2)}
+
+        def cast_w1(engine, g, d):
+            dst = w1_bf[(g, d)][:].rearrange("p (t m j) -> p m j t", t=2, j=PACK)
+            src = w1_raw[g][:].rearrange("p j (m t) -> p m j t", t=PACK)[:, :, :, 2 * d : 2 * d + 2]
+            cast_copy(engine, dst, src)
+
+        def quantize_w1(g, d):
+            quantize(w1_codes[(g, d)][:], w1_scales[(g, d)][:], w1_bf[(g, d)][:])
+
+        banks = {(t, h): psum.tile([P, HALF], F32, name="bank_%d_%d" % (t, h)) for t in range(PACK) for h in range(2)}
+
+        def product1(g, t, h):
+            d, r = divmod(t, 2)
+            cols = slice(r * P, (r + 1) * P)
+            nc.tensor.matmul_mx(
+                out=banks[(t, h)][:],
+                lhsT=w1_codes[(g, d)][:, cols].bitcast(FP8X4),
+                lhsT_scale=w1_scales[(g, d)][:, cols],
+                rhs=x_codes[(g, h)][:].bitcast(FP8X4),
+                rhs_scale=x_scales[(g, h)][:],
+                start=(g == 0),
+                stop=(g == 1),
+            )
+
+        for g, u, share in ((0, 0, 704), (0, 1, 704), (1, 0, 192)):
+            cast_x("s", g, u, 0, 0, 1024)
+            cast_x("v", g, u, 1024, 1024, 1024 + share)
+            cast_x("s", g, u, 1024, 1024 + share, 2048)
+            for q in range(4):
+                gather(g, u, q)
+            if (g, u) == (0, 1):
+                for q in range(4):
+                    weave("s" if q == 0 else "v", 0, q)
+                for h in range(2):
+                    quantize_x(0, h)
+
+        cast_x("s", 1, 1, 0, 0, 1024)
+        cast_w1("v", 0, 0)
+        cast_w1("s", 0, 1)
+        quantize_w1(0, 0)
+        quantize_w1(0, 1)
+        for t in range(PACK):
+            product1(0, t, 0)
+        cast_x("s", 1, 1, 1024, 1024, 1536)
+        cast_x("v", 1, 1, 1536, 1536, 1536 + 352)
+        cast_x("s", 1, 1, 1536, 1536 + 352, 2048)
+        w2_bf = picked[(1, 3)][:, 1, :].bitcast(BF16)
+        w2_codes = sbuf("w2_codes", [P, N], U32)
+        w2_scales = x_scales[(0, 1)][4:P, 0:N]
+        cast_copy(
+            "s",
+            w2_bf.rearrange("p (c i j) -> p c j i", i=4, j=PACK),
+            w2_raw[:].rearrange("p j (c i) -> p c j i", i=4),
+        )
+        for q in range(4):
+            if q == 3:
+                quantize(w2_codes[:], w2_scales, w2_bf)
+            gather(1, 1, q)
+            weave("s" if q < 3 else "v", 1, q)
+        for t in range(PACK):
+            product1(0, t, 1)
+        quantize_x(1, 0)
+        cast_w1("s", 1, 0)
+        cast_w1("s", 1, 1)
+        quantize_w1(1, 0)
+        x_codes[(1, 1)] = sbuf("w1_bf_1_0", [P, HALF], U32)
+        quantize_x(1, 1)
+        quantize_w1(1, 1)
+
+        hidden = [sbuf("hidden_%d" % t, [P, S], F32) for t in range(PACK)]
+        part = sbuf("part", [P, PACK], F32)
+        sums = sbuf("sums", [P, PACK], F32)
+
+        def relu_out(t, h):
+            dst = hidden[t][:, h * HALF : (h + 1) * HALF]
+            if h == 0:
+                nc.scalar.activation(out=dst, in_=banks[(t, h)][:], func=ACT.Relu, accum_out=part[:, t : t + 1])
+            else:
+                nc.vector.tensor_scalar(
+                    out=dst,
+                    in0=banks[(t, h)][:],
+                    scalar1=0.0,
+                    scalar2=part[:, t : t + 1],
+                    op0=ALU.max,
+                    op1=ALU.add,
+                    accum_out=sums[:, t : t + 1],
+                )
+
+        order = ((0, 0), (1, 0), (0, 1), (1, 1), (2, 0), (2, 1), (3, 0), (3, 1))
+        for t, h in order:
+            product1(1, t, h)
+        for t in range(PACK):
+            relu_out(t, 0)
+            relu_out(t, 1)
+
+        centred = [sbuf("centred_%d" % h, [P, PACK, HALF], BF16) for h in range(2)]
+
+        def centre(engine, t, h):
+            dst = centred[h][:, t, :]
+            src = hidden[t][:, h * HALF : (h + 1) * HALF]
+            if engine == "v":
+                nc.vector.tensor_scalar(
+                    out=dst, in0=src, scalar1=-float(S), scalar2=sums[:, t : t + 1], op0=ALU.mult, op1=ALU.add
+                )
+            else:
+                nc.scalar.activation(out=dst, in_=src, func=ACT.Identity, scale=-float(S), bias=sums[:, t : t + 1])
+
+        for engine, t, h in (
+            ("s", 0, 0), ("s", 1, 0), ("v", 2, 0), ("v", 3, 0), ("s", 0, 1), ("v", 1, 1), ("v", 2, 1), ("v", 3, 1),
+        ):
+            centre(engine, t, h)
+
+        z_bf = [sbuf("z_bf_%d" % q, [P, PACK * QUART], BF16) for q in range(4)]
+        z_codes = [sbuf("z_codes_%d" % q, [P, QUART], U32) for q in range(4)]
+        z_scales = [sbuf("z_scales_%d" % q, [P, QUART], U8) for q in range(4)]
+        result = [sbuf("result_%d" % q, [P, QUART], F32) for q in range(4)]
+
+        def interleave(engine, q, a=0, b=QUART):
+            h, r = divmod(q, 2)
+            dst = z_bf[q][:, PACK * a : PACK * b].rearrange("p (c i t) -> p c t i", i=4, t=PACK)
+            src = centred[h][:, :, r * QUART + a : r * QUART + b].rearrange("p t (c i) -> p c t i", i=4)
+            if engine == "v":
+                nc.vector.tensor_copy(out=dst, in_=src)
+            else:
+                nc.scalar.copy(out=dst, in_=src)
+
+        def product2(engine, q):
+            quantize(z_codes[q][:], z_scales[q][:], z_bf[q][:])
+            acc = psum.tile([P, HALF], F32, name="bank_%d_%d" % order[q])
+            nc.tensor.matmul_mx(
+                out=acc[:, 0:QUART],
+                lhsT=w2_codes[:].bitcast(FP8X4),
+                lhsT_scale=w2_scales,
+                rhs=z_codes[q][:].bitcast(FP8X4),
+                rhs_scale=z_scales[q][:],
+                start=True,
+                stop=True,
+            )
+            if engine == "v":
+                nc.vector.tensor_scalar(
+                    out=result[q][:], in0=acc[:, 0:QUART], scalar1=-1.0 / S, scalar2=None, op0=ALU.mult
+                )
+            else:
+                nc.scalar.activation(out=result[q][:], in_=acc[:, 0:QUART], func=ACT.Copy, scale=-1.0 / S)
+            nc.sync.dma_start(out=out[:, q * QUART : (q + 1) * QUART], in_=result[q][:])
+
+        interleave("s", 0)
+        interleave("s", 1)
+        interleave("v", 2)
+        interleave("v", 3, 0, 128)
+        interleave("s", 3, 128, 256)
+        product2("s", 0)
+        product2("s", 1)
+        product2("s", 2)
+        product2("v", 3)

@@ -46,11 +46,9 @@ def tile_picked_deepset_relu_e_kernel(tc, xT, w1, w2, offs, out):
         w1_raw = [sbuf("w1_raw_%d" % g, [P, PACK, H], F32) for g in range(2)]
         w2_raw = sbuf("w2_raw", [P, PACK, N], F32)
 
-        load_x(0, 0, 0, 1024)
+        load_x(0, 0, 0, 2048)
         nc.sync.dma_start(offsets[:], offs)
-        load_x(0, 0, 1024, 2048)
-        load_x(0, 1, 0, 1024)
-        load_x(0, 1, 1024, 2048)
+        load_x(0, 1, 0, 2048)
         load_x(1, 0, 0, 1024)
         load_x(1, 0, 1024, 2048)
         load_x(1, 1, 0, 1024)
@@ -73,19 +71,22 @@ def tile_picked_deepset_relu_e_kernel(tc, xT, w1, w2, offs, out):
             src = x_raw[(g, u, t0)][:, :, a - t0 : b - t0].rearrange("p e t -> p t e")
             cast_copy(engine, dst, src)
 
-        picked = {(g, q): sbuf("picked_%d_%d" % (g, q), [P, 2, QUART], U32) for g in range(2) for q in range(4)}
+        width = (HALF, QUART)
+        picked = {
+            (g, q): sbuf("picked_%d_%d" % (g, q), [P, 2, width[g]], U32) for g in range(2) for q in range(S // width[g])
+        }
         woven = {(g, h): sbuf("woven_%d_%d" % (g, h), [P, PACK * HALF], BF16) for g in range(2) for h in range(2)}
         x_codes = {(g, h): sbuf("x_codes_%d_%d" % (g, h), [P, HALF], U32) for g, h in ((0, 0), (0, 1), (1, 0))}
         x_scales = {(g, h): sbuf("x_scales_%d_%d" % (g, h), [P, HALF], U8) for g in range(2) for h in range(2)}
 
         def gather(g, u, q):
             window = pairs[(g, u)][:].bitcast(U32)
-            cols = QUART // 16
+            cols = width[g] // 16
             nc.vector.tensor_copy(out=picked[(g, q)][:, u, :], in_=window.indirect(offsets[:, q * cols : (q + 1) * cols]))
 
         def weave(engine, g, q):
-            h, r = divmod(q, 2)
-            dst = woven[(g, h)][:, r * PACK * QUART : (r + 1) * PACK * QUART]
+            h, r = divmod(q, HALF // width[g])
+            dst = woven[(g, h)][:, r * PACK * width[g] : (r + 1) * PACK * width[g]]
             src = picked[(g, q)][:]
             if engine == "v":
                 nc.vector.tensor_copy(
@@ -131,17 +132,19 @@ def tile_picked_deepset_relu_e_kernel(tc, xT, w1, w2, offs, out):
                 stop=(g == 1),
             )
 
-        for g, u, share in ((0, 0, 704), (0, 1, 704), (1, 0, 192)):
-            cast_x("s", g, u, 0, 0, 1024)
-            cast_x("v", g, u, 1024, 1024, 1024 + share)
-            cast_x("s", g, u, 1024, 1024 + share, 2048)
-            for q in range(4):
-                gather(g, u, q)
-            if (g, u) == (0, 1):
-                for q in range(4):
-                    weave("s" if q == 0 else "v", 0, q)
-                for h in range(2):
-                    quantize_x(0, h)
+        for u in range(2):
+            cast_x("v", 0, u, 0, 0, 1376)
+            cast_x("s", 0, u, 0, 1376, 2048)
+            for q in range(2):
+                gather(0, u, q)
+        for q in range(2):
+            weave("v", 0, q)
+        for h in range(2):
+            quantize_x(0, h)
+        cast_x("s", 1, 0, 0, 0, 1024)
+        cast_x("s", 1, 0, 1024, 1024, 2048)
+        for q in range(4):
+            gather(1, 0, q)
 
         cast_x("s", 1, 1, 0, 0, 1024)
         cast_w1("v", 0, 0)
@@ -211,11 +214,15 @@ def tile_picked_deepset_relu_e_kernel(tc, xT, w1, w2, offs, out):
                 nc.vector.tensor_scalar(
                     out=dst, in0=src, scalar1=-float(S), scalar2=sums[:, t : t + 1], op0=ALU.mult, op1=ALU.add
                 )
+            elif engine == "g":
+                nc.gpsimd.tensor_scalar(
+                    out=dst, in0=src, scalar1=-float(S), scalar2=sums[:, t : t + 1], op0=ALU.mult, op1=ALU.add
+                )
             else:
                 nc.scalar.activation(out=dst, in_=src, func=ACT.Identity, scale=-float(S), bias=sums[:, t : t + 1])
 
         for engine, t, h in (
-            ("s", 0, 0), ("s", 1, 0), ("v", 2, 0), ("v", 3, 0), ("s", 0, 1), ("v", 1, 1), ("v", 2, 1), ("v", 3, 1),
+            ("g", 0, 0), ("g", 0, 1), ("s", 1, 0), ("s", 1, 1), ("v", 2, 0), ("v", 3, 0), ("v", 2, 1), ("v", 3, 1),
         ):
             centre(engine, t, h)
 
@@ -256,9 +263,9 @@ def tile_picked_deepset_relu_e_kernel(tc, xT, w1, w2, offs, out):
         interleave("s", 0)
         interleave("s", 1)
         interleave("v", 2)
-        interleave("v", 3, 0, 128)
-        interleave("s", 3, 128, 256)
+        interleave("v", 3, 0, 192)
+        interleave("s", 3, 192, 256)
         product2("s", 0)
-        product2("s", 1)
         product2("s", 2)
+        product2("s", 1)
         product2("v", 3)

@@ -75,7 +75,10 @@ def tile_picked_deepset_relu_e_kernel(tc, xT, w1, w2, offs, out):
         picked = {
             (g, q): sbuf("picked_%d_%d" % (g, q), [P, 2, width[g]], U32) for g in range(2) for q in range(S // width[g])
         }
-        woven = {(g, h): sbuf("woven_%d_%d" % (g, h), [P, PACK * HALF], BF16) for g in range(2) for h in range(2)}
+        woven = {(0, h): sbuf("woven_0_%d" % h, [P, PACK * HALF], BF16)[:] for h in range(2)}
+        woven_late = sbuf("woven_1", [P, 3 * PACK * QUART], BF16)
+        woven[(1, 0)] = woven_late[:, 0 : PACK * HALF]
+        woven[(1, 1)] = woven_late[:, PACK * QUART : 3 * PACK * QUART]
         x_codes = {(g, h): sbuf("x_codes_%d_%d" % (g, h), [P, HALF], U32) for g, h in ((0, 0), (0, 1), (1, 0))}
         x_scales = {(g, h): sbuf("x_scales_%d_%d" % (g, h), [P, HALF], U8) for g in range(2) for h in range(2)}
 
@@ -103,7 +106,7 @@ def tile_picked_deepset_relu_e_kernel(tc, xT, w1, w2, offs, out):
             nc.vector.quantize_mx(out=codes.bitcast(FP8X4), scales=scales, in_=values)
 
         def quantize_x(g, h):
-            quantize(x_codes[(g, h)][:], x_scales[(g, h)][:], woven[(g, h)][:])
+            quantize(x_codes[(g, h)][:], x_scales[(g, h)][:], woven[(g, h)])
 
         w1_bf = {(g, d): sbuf("w1_bf_%d_%d" % (g, d), [P, 2 * P * PACK], BF16) for g in range(2) for d in range(2)}
         w1_codes = {(g, d): sbuf("w1_codes_%d_%d" % (g, d), [P, 2 * P], U32) for g in range(2) for d in range(2)}
@@ -156,7 +159,7 @@ def tile_picked_deepset_relu_e_kernel(tc, xT, w1, w2, offs, out):
         cast_x("s", 1, 1, 1024, 1024, 1536)
         cast_x("v", 1, 1, 1536, 1536, 1536 + 352)
         cast_x("s", 1, 1, 1536, 1536 + 352, 2048)
-        w2_bf = picked[(1, 3)][:, 1, :].bitcast(BF16)
+        w2_bf = picked[(1, 2)][:, 1, :].bitcast(BF16)
         w2_codes = sbuf("w2_codes", [P, N], U32)
         w2_scales = x_scales[(0, 1)][4:P, 0:N]
         cast_copy(
@@ -164,14 +167,15 @@ def tile_picked_deepset_relu_e_kernel(tc, xT, w1, w2, offs, out):
             w2_bf.rearrange("p (c i j) -> p c j i", i=4, j=PACK),
             w2_raw[:].rearrange("p j (c i) -> p c j i", i=4),
         )
-        for q in range(4):
-            if q == 3:
-                quantize(w2_codes[:], w2_scales, w2_bf)
+        for q in (0, 1, 3):
             gather(1, 1, q)
-            weave("s" if q < 3 else "v", 1, q)
+            weave("s", 1, q)
+        quantize(w2_codes[:], w2_scales, w2_bf)
+        gather(1, 1, 2)
         for t in range(PACK):
             product1(0, t, 1)
         quantize_x(1, 0)
+        weave("v", 1, 2)
         cast_w1("s", 1, 0)
         cast_w1("s", 1, 1)
         quantize_w1(1, 0)
@@ -226,25 +230,27 @@ def tile_picked_deepset_relu_e_kernel(tc, xT, w1, w2, offs, out):
         ):
             centre(engine, t, h)
 
-        z_bf = [sbuf("z_bf_%d" % q, [P, PACK * QUART], BF16) for q in range(4)]
-        z_codes = [sbuf("z_codes_%d" % q, [P, QUART], U32) for q in range(4)]
-        z_scales = [sbuf("z_scales_%d" % q, [P, QUART], U8) for q in range(4)]
-        result = [sbuf("result_%d" % q, [P, QUART], F32) for q in range(4)]
+        pieces = ((0, 256), (256, 512), (512, 768), (768, 896), (896, 1024))
+        z_bf = [sbuf("z_bf_%d" % q, [P, PACK * (b - a)], BF16) for q, (a, b) in enumerate(pieces)]
+        z_codes = [sbuf("z_codes_%d" % q, [P, b - a], U32) for q, (a, b) in enumerate(pieces)]
+        z_scales = [sbuf("z_scales_%d" % q, [P, b - a], U8) for q, (a, b) in enumerate(pieces)]
+        result = [sbuf("result_%d" % q, [P, b - a], F32) for q, (a, b) in enumerate(pieces)]
 
-        def interleave(engine, q, a=0, b=QUART):
-            h, r = divmod(q, 2)
-            dst = z_bf[q][:, PACK * a : PACK * b].rearrange("p (c i t) -> p c t i", i=4, t=PACK)
-            src = centred[h][:, :, r * QUART + a : r * QUART + b].rearrange("p t (c i) -> p c t i", i=4)
+        def interleave(engine, q, lo, hi):
+            h, first = divmod(pieces[q][0], HALF)
+            dst = z_bf[q][:, PACK * lo : PACK * hi].rearrange("p (c i t) -> p c t i", i=4, t=PACK)
+            src = centred[h][:, :, first + lo : first + hi].rearrange("p t (c i) -> p c t i", i=4)
             if engine == "v":
                 nc.vector.tensor_copy(out=dst, in_=src)
             else:
                 nc.scalar.copy(out=dst, in_=src)
 
         def product2(engine, q):
+            a, b = pieces[q]
             quantize(z_codes[q][:], z_scales[q][:], z_bf[q][:])
             acc = psum.tile([P, HALF], F32, name="bank_%d_%d" % order[q])
             nc.tensor.matmul_mx(
-                out=acc[:, 0:QUART],
+                out=acc[:, 0 : b - a],
                 lhsT=w2_codes[:].bitcast(FP8X4),
                 lhsT_scale=w2_scales,
                 rhs=z_codes[q][:].bitcast(FP8X4),
@@ -254,18 +260,20 @@ def tile_picked_deepset_relu_e_kernel(tc, xT, w1, w2, offs, out):
             )
             if engine == "v":
                 nc.vector.tensor_scalar(
-                    out=result[q][:], in0=acc[:, 0:QUART], scalar1=-1.0 / S, scalar2=None, op0=ALU.mult
+                    out=result[q][:], in0=acc[:, 0 : b - a], scalar1=-1.0 / S, scalar2=None, op0=ALU.mult
                 )
             else:
-                nc.scalar.activation(out=result[q][:], in_=acc[:, 0:QUART], func=ACT.Copy, scale=-1.0 / S)
-            nc.sync.dma_start(out=out[:, q * QUART : (q + 1) * QUART], in_=result[q][:])
+                nc.scalar.activation(out=result[q][:], in_=acc[:, 0 : b - a], func=ACT.Copy, scale=-1.0 / S)
+            nc.sync.dma_start(out=out[:, a:b], in_=result[q][:])
 
-        interleave("s", 0)
-        interleave("s", 1)
-        interleave("v", 2)
-        interleave("v", 3, 0, 192)
-        interleave("s", 3, 192, 256)
+        interleave("s", 0, 0, 256)
+        interleave("v", 1, 0, 256)
+        interleave("s", 2, 0, 256)
+        interleave("v", 3, 0, 128)
+        interleave("v", 4, 0, 64)
+        interleave("s", 4, 64, 128)
         product2("s", 0)
-        product2("s", 2)
         product2("s", 1)
-        product2("v", 3)
+        product2("s", 3)
+        product2("v", 2)
+        product2("s", 4)

from contextlib import ExitStack

import concourse.mybir as mybir

K, T, S, H, N = 1024, 2048, 1024, 512, 128
FLOPS = 2 * K * H * S + 2 * H * N * S

F32 = mybir.dt.float32
BF16 = mybir.dt.bfloat16
I32 = mybir.dt.int32
U32 = mybir.dt.uint32
U16 = mybir.dt.uint16
U8 = mybir.dt.uint8
FP8X4 = mybir.dt.float8_e4m3fn_x4
ALU = mybir.AluOpType
ACT = mybir.ActivationFunctionType

P = 128
PACK = 4
HALF = 512
QUART = 256


def tile_picked_deepset_relu_e_kernel(tc, xT, w1, w2, offs, out):
    nc = tc.nc
    x_rows = xT.rearrange("(g p u e) t -> g u p e t", g=2, p=P, u=2, e=2)
    w1_rows = w1.rearrange("(g p j) c -> g p j c", g=2, p=P, j=PACK)
    w2_rows = w2.rearrange("(p j) n -> p j n", j=PACK)

    with ExitStack() as ctx:
        keep = ctx.enter_context(tc.tile_pool(name="keep", bufs=1))
        psum = ctx.enter_context(tc.psum_pool(name="psum", bufs=1))

        def sbuf(name, shape, dtype):
            return keep.tile(shape, dtype, name=name, align_bytes=64)

        offsets = keep.tile([P, S // 16], U16, name="offsets")

        x_raw = {}

        def load_x(g, u, t0, t1):
            raw = sbuf("x_raw_%d_%d_%d" % (g, u, t0), [P, 2, t1 - t0], F32)
            nc.sync.dma_start(out=raw[:], in_=x_rows[g, u][:, :, t0:t1])
            x_raw[(g, u, t0)] = raw

        w1_raw = [sbuf("w1_raw_%d" % g, [P, PACK, H], F32) for g in range(2)]
        w2_raw = sbuf("w2_raw", [P, PACK, N], F32)

        load_x(0, 0, 0, 2048)
        nc.sync.dma_start(offsets[:], offs)
        load_x(0, 1, 0, 2048)
        load_x(1, 0, 0, 1024)
        load_x(1, 0, 1024, 2048)
        load_x(1, 1, 0, 1024)
        nc.sync.dma_start(out=w1_raw[0][:], in_=w1_rows[0])
        load_x(1, 1, 1024, 1536)
        load_x(1, 1, 1536, 2048)
        nc.sync.dma_start(out=w2_raw[:], in_=w2_rows)
        nc.sync.dma_start(out=w1_raw[1][:], in_=w1_rows[1])

        pairs = {(g, u): sbuf("pairs_%d_%d" % (g, u), [P, 2 * T], BF16) for g in range(2) for u in range(2)}

        def cast_copy(engine, dst, src):
            if engine == "v":
                nc.vector.tensor_copy(out=dst, in_=src)
            else:
                nc.scalar.activation(out=dst, in_=src, func=ACT.Copy)

        def cast_x(engine, g, u, t0, a, b):
            dst = pairs[(g, u)][:, 2 * a : 2 * b].rearrange("p (t e) -> p t e", e=2)
            src = x_raw[(g, u, t0)][:, :, a - t0 : b - t0].rearrange("p e t -> p t e")
            cast_copy(engine, dst, src)

        width = (HALF, QUART)
        picked = {
            (g, q): sbuf("picked_%d_%d" % (g, q), [P, 2, width[g]], U32) for g in range(2) for q in range(S // width[g])
        }
        woven = {(0, h): sbuf("woven_0_%d" % h, [P, PACK * HALF], BF16)[:] for h in range(2)}
        woven_late = sbuf("woven_1", [P, 3 * PACK * QUART], BF16)
        woven[(1, 0)] = woven_late[:, 0 : PACK * HALF]
        woven[(1, 1)] = woven_late[:, PACK * QUART : 3 * PACK * QUART]
        x_codes = {(g, h): sbuf("x_codes_%d_%d" % (g, h), [P, HALF], U32) for g, h in ((0, 0), (0, 1), (1, 0))}
        x_scales = {(g, h): sbuf("x_scales_%d_%d" % (g, h), [P, HALF], U8) for g in range(2) for h in range(2)}

        def gather(g, u, q):
            window = pairs[(g, u)][:].bitcast(U32)
            cols = width[g] // 16
            nc.vector.tensor_copy(out=picked[(g, q)][:, u, :], in_=window.indirect(offsets[:, q * cols : (q + 1) * cols]))

        def weave(engine, g, q):
            h, r = divmod(q, HALF // width[g])
            dst = woven[(g, h)][:, r * PACK * width[g] : (r + 1) * PACK * width[g]]
            src = picked[(g, q)][:]
            if engine == "v":
                nc.vector.tensor_copy(
                    out=dst.bitcast(I32).rearrange("p (n u) -> p n u", u=2),
                    in_=src.bitcast(I32).rearrange("p u n -> p n u"),
                )
            else:
                nc.scalar.copy(
                    out=dst.bitcast(U32).rearrange("p (n u) -> p n u", u=2),
                    in_=src.rearrange("p u n -> p n u"),
                )

        def quantize(codes, scales, values):
            nc.vector.quantize_mx(out=codes.bitcast(FP8X4), scales=scales, in_=values)

        def quantize_x(g, h):
            quantize(x_codes[(g, h)][:], x_scales[(g, h)][:], woven[(g, h)])

        w1_bf = {(g, d): sbuf("w1_bf_%d_%d" % (g, d), [P, 2 * P * PACK], BF16) for g in range(2) for d in range(2)}
        w1_codes = {(g, d): sbuf("w1_codes_%d_%d" % (g, d), [P, 2 * P], U32) for g in range(2) for d in range(2)}
        w1_scales = {(g, d): sbuf("w1_scales_%d_%d" % (g, d), [P, 2 * P], U8) for g in range(2) for d in range(2)}

        def cast_w1(engine, g, d):
            dst = w1_bf[(g, d)][:].rearrange("p (t m j) -> p m j t", t=2, j=PACK)
            src = w1_raw[g][:].rearrange("p j (m t) -> p m j t", t=PACK)[:, :, :, 2 * d : 2 * d + 2]
            cast_copy(engine, dst, src)

        def quantize_w1(g, d):
            quantize(w1_codes[(g, d)][:], w1_scales[(g, d)][:], w1_bf[(g, d)][:])

        banks = {(t, h): psum.tile([P, HALF], F32, name="bank_%d_%d" % (t, h)) for t in range(PACK) for h in range(2)}

        def product1(g, t, h):
            d, r = divmod(t, 2)
            cols = slice(r * P, (r + 1) * P)
            nc.tensor.matmul_mx(
                out=banks[(t, h)][:],
                lhsT=w1_codes[(g, d)][:, cols].bitcast(FP8X4),
                lhsT_scale=w1_scales[(g, d)][:, cols],
                rhs=x_codes[(g, h)][:].bitcast(FP8X4),
                rhs_scale=x_scales[(g, h)][:],
                start=(g == 0),
                stop=(g == 1),
            )

        for u in range(2):
            cast_x("v", 0, u, 0, 0, 1376)
            cast_x("s", 0, u, 0, 1376, 2048)
            for q in range(2):
                gather(0, u, q)
        for q in range(2):
            weave("v", 0, q)
        for h in range(2):
            quantize_x(0, h)
        cast_x("s", 1, 0, 0, 0, 1024)
        cast_x("s", 1, 0, 1024, 1024, 2048)
        for q in range(4):
            gather(1, 0, q)

        cast_x("s", 1, 1, 0, 0, 1024)
        cast_w1("v", 0, 0)
        cast_w1("s", 0, 1)
        quantize_w1(0, 0)
        quantize_w1(0, 1)
        for t in range(PACK):
            product1(0, t, 0)
        cast_x("s", 1, 1, 1024, 1024, 1536)
        cast_x("v", 1, 1, 1536, 1536, 1536 + 352)
        cast_x("s", 1, 1, 1536, 1536 + 352, 2048)
        w2_bf = picked[(1, 2)][:, 1, :].bitcast(BF16)
        w2_codes = sbuf("w2_codes", [P, N], U32)
        w2_scales = x_scales[(0, 1)][4:P, 0:N]
        cast_copy(
            "s",
            w2_bf.rearrange("p (c i j) -> p c j i", i=4, j=PACK),
            w2_raw[:].rearrange("p j (c i) -> p c j i", i=4),
        )
        for q in (0, 1, 3):
            gather(1, 1, q)
            weave("s", 1, q)
        quantize(w2_codes[:], w2_scales, w2_bf)
        gather(1, 1, 2)
        for t in range(PACK):
            product1(0, t, 1)
        quantize_x(1, 0)
        weave("v", 1, 2)
        cast_w1("s", 1, 0)
        cast_w1("s", 1, 1)
        quantize_w1(1, 0)
        x_codes[(1, 1)] = sbuf("w1_bf_1_0", [P, HALF], U32)
        quantize_x(1, 1)
        quantize_w1(1, 1)

        hidden = [sbuf("hidden_%d" % t, [P, S], F32) for t in range(PACK)]
        part = sbuf("part", [P, PACK], F32)
        sums = sbuf("sums", [P, PACK], F32)

        def relu_out(t, h):
            dst = hidden[t][:, h * HALF : (h + 1) * HALF]
            if h == 0:
                nc.scalar.activation(out=dst, in_=banks[(t, h)][:], func=ACT.Relu, accum_out=part[:, t : t + 1])
            else:
                nc.vector.tensor_scalar(
                    out=dst,
                    in0=banks[(t, h)][:],
                    scalar1=0.0,
                    scalar2=part[:, t : t + 1],
                    op0=ALU.max,
                    op1=ALU.add,
                    accum_out=sums[:, t : t + 1],
                )

        order = ((0, 0), (1, 0), (0, 1), (1, 1), (2, 0), (2, 1), (3, 0), (3, 1))
        for t, h in order:
            product1(1, t, h)
        for t in range(PACK):
            relu_out(t, 0)
            relu_out(t, 1)

        centred = [sbuf("centred_%d" % h, [P, PACK, HALF], BF16) for h in range(2)]

        def centre(engine, t, h):
            dst = centred[h][:, t, :]
            src = hidden[t][:, h * HALF : (h + 1) * HALF]
            if engine == "v":
                nc.vector.tensor_scalar(
                    out=dst, in0=src, scalar1=-float(S), scalar2=sums[:, t : t + 1], op0=ALU.mult, op1=ALU.add
                )
            elif engine == "g":
                nc.gpsimd.tensor_scalar(
                    out=dst, in0=src, scalar1=-float(S), scalar2=sums[:, t : t + 1], op0=ALU.mult, op1=ALU.add
                )
            else:
                nc.scalar.activation(out=dst, in_=src, func=ACT.Identity, scale=-float(S), bias=sums[:, t : t + 1])

        for engine, t, h in (
            ("g", 0, 0), ("g", 0, 1), ("s", 1, 0), ("s", 1, 1), ("v", 2, 0), ("v", 3, 0), ("v", 2, 1), ("v", 3, 1),
        ):
            centre(engine, t, h)

        pieces = ((0, 256), (256, 512), (512, 768), (768, 896), (896, 1024))
        z_bf = [sbuf("z_bf_%d" % q, [P, PACK * (b - a)], BF16) for q, (a, b) in enumerate(pieces)]
        z_codes = [sbuf("z_codes_%d" % q, [P, b - a], U32) for q, (a, b) in enumerate(pieces)]
        z_scales = [sbuf("z_scales_%d" % q, [P, b - a], U8) for q, (a, b) in enumerate(pieces)]
        result = [sbuf("result_%d" % q, [P, b - a], F32) for q, (a, b) in enumerate(pieces)]

        def interleave(engine, q, lo, hi):
            h, first = divmod(pieces[q][0], HALF)
            dst = z_bf[q][:, PACK * lo : PACK * hi].rearrange("p (c i t) -> p c t i", i=4, t=PACK)
            src = centred[h][:, :, first + lo : first + hi].rearrange("p t (c i) -> p c t i", i=4)
            if engine == "v":
                nc.vector.tensor_copy(out=dst, in_=src)
            else:
                nc.scalar.copy(out=dst, in_=src)

        def product2(engine, q):
            a, b = pieces[q]
            quantize(z_codes[q][:], z_scales[q][:], z_bf[q][:])
            acc = psum.tile([P, HALF], F32, name="bank_%d_%d" % order[q])
            nc.tensor.matmul_mx(
                out=acc[:, 0 : b - a],
                lhsT=w2_codes[:].bitcast(FP8X4),
                lhsT_scale=w2_scales,
                rhs=z_codes[q][:].bitcast(FP8X4),
                rhs_scale=z_scales[q][:],
                start=True,
                stop=True,
            )
            if engine == "v":
                nc.vector.tensor_scalar(
                    out=result[q][:], in0=acc[:, 0 : b - a], scalar1=-1.0 / S, scalar2=None, op0=ALU.mult
                )
            else:
                nc.scalar.activation(out=result[q][:], in_=acc[:, 0 : b - a], func=ACT.Copy, scale=-1.0 / S)
            nc.sync.dma_start(out=out[:, a:b], in_=result[q][:])

        interleave("s", 0, 0, 256)
        interleave("v", 1, 0, 256)
        interleave("s", 2, 0, 256)
        interleave("v", 3, 0, 128)
        interleave("v", 4, 0, 64)
        interleave("s", 4, 64, 128)
        product2("s", 0)
        product2("s", 1)
        product2("s", 3)
        product2("v", 2)
        product2("s", 4)
